import numpy as np
CORES = [6,10,22,26,38,42,54,58]
N = 8
COUNTS = [[0,128,64,128,128,128,512,0],[128,0,64,64,64,128,512,0],[64,64,0,128,64,0,512,128],[0,64,0,0,128,128,512,128],[64,0,128,64,0,64,512,64],[64,128,0,64,64,0,512,64],[0,64,64,64,0,0,0,0],[64,64,0,128,128,0,512,0]]
XW, YW = 1088, 3584
def setup_inputs(rng):
    return {"x": rng.standard_normal((N, 128, XW), dtype=np.float32)}
def reference(x):
    y = np.full((N, 128, YW), np.nan, x.dtype)
    fill = [0] * N
    for s in range(N):
        o = 0
        for d in range(N):
            c = COUNTS[s][d]
            y[d][:, fill[d]:fill[d] + c] = x[s][:, o:o + c]
            o += c; fill[d] += c
    return {"y": y}

@@ -1,0 +1,154 @@
+from concourse.bass import DstId, RemoteDMATransfer
+
+HOT = 6
+NQ = 4
+RELAY = {0: (62, 2), 2: (62, 2), 3: (63, 2), 4: (63, 1), 1: (59, 2), 5: (59, 1)}
+HOTMASK = [0x03, 0x0C, 0x30, 0xC0]
+MASKS = {1: [0xFF], 2: [0x0F, 0xF0], 3: [0x0F, 0x30, 0xC0], 4: [0x03, 0x0C, 0x30, 0xC0]}
+
+SCRATCH = {
+    "hs": ("dram", [NQ, 128, 128], "float32"),
+    "xs": ("sbuf", [128, 1088], "float32"),
+    "land": ("sbuf", [128, 640], "float32"),
+}
+for i in range(7):
+    SCRATCH["hl%d" % i] = ("dram", [NQ, 128, 128], "float32")
+
+SEMAPHORES = ["lh", "ln", "snt", "nh", "st", "sg"] + ["hd%d" % i for i in range(7)] + ["hr%d" % i for i in range(7)]
+
+
+def bits(m):
+    return bin(m).count("1")
+
+
+def nh_calls(C, s):
+    groups = {}
+    for d in range(len(C)):
+        if d != HOT and C[s][d] > 0:
+            groups.setdefault(C[s][d], []).append(d)
+    calls = []
+    for w in sorted(groups, reverse=True):
+        ds = groups[w]
+        calls.append(list(zip(ds, MASKS[len(ds)])))
+    return calls
+
+
+def rank_program(g, core, T, topo):
+    C = T.tables["COUNTS"]
+    cores = T.cores
+    n = len(cores)
+    hotcore = cores[HOT]
+    rank = T.rank_of(core)
+    srcs = [s for s in range(n) if C[s][HOT] > 0]
+    pos = {s: i for i, s in enumerate(srcs)}
+    W = C[srcs[0]][HOT]
+
+    def did(c):
+        a = topo.addr(c)
+        return DstId(rid=a[0], pnc=a[1])
+
+    def send(trs):
+        g.remote_dma_fused(trs, local_sem=T.sem.snt)
+        return sum(bits(t[0]) for t in trs) if False else 0
+
+    if rank is None:
+        mine = [s for s in srcs if s in RELAY and RELAY[s][0] == core]
+        if not mine:
+            return
+        sent = 0
+        for s in mine:
+            k = RELAY[s][1]
+            p = pos[s]
+            buf = T["hl%d" % p]
+            g.wait_ge(T.sem["hd%d" % p], 2 * k)
+            trs = []
+            for i in range(k):
+                j = NQ - k + i
+                trs.append(RemoteDMATransfer(dst_ids=[did(hotcore)], dma_engine_mask=MASKS[k][i],
+                                             remote_sem=T.sem["hr%d" % p], src=buf[j], dst=buf[j]))
+            g.remote_dma_fused(trs, local_sem=T.sem.snt)
+            sent += 8
+        g.wait_ge(T.sem.snt, sent)
+        return
+
+    xoff = [sum(C[rank][:d]) for d in range(n)]
+    tot = sum(C[rank])
+    sent = 0
+
+    nload = 0
+    if rank != HOT:
+        h = xoff[HOT]
+        g.sync.dma_start(T.hs[0:2], T.x[0:64, h:h + W]).then_inc(T.sem.lh, 16)
+        g.scalar.dma_start(T.hs[2:4], T.x[64:128, h:h + W]).then_inc(T.sem.lh, 16)
+        if h > 0:
+            g.sync.dma_start(T.xs[:, 0:h], T.x[:, 0:h]).then_inc(T.sem.ln, 16)
+            nload += 16
+        if tot > h + W:
+            g.scalar.dma_start(T.xs[:, h + W:tot], T.x[:, h + W:tot]).then_inc(T.sem.ln, 16)
+            nload += 16
+        p = pos[rank]
+        k = RELAY[rank][1] if rank in RELAY else 0
+        g.wait_ge(T.sem.lh, 32)
+        trs = []
+        for j in range(NQ):
+            to = hotcore if j < NQ - k else RELAY[rank][0]
+            trs.append(RemoteDMATransfer(dst_ids=[did(to)], dma_engine_mask=HOTMASK[j],
+                                         remote_sem=T.sem["hd%d" % p], src=T.hs[j], dst=T["hl%d" % p][j]))
+            sent += bits(HOTMASK[j])
+        g.remote_dma_fused(trs, local_sem=T.sem.snt)
+    else:
+        g.sync.dma_start(T.xs[:, 0:tot], T.x[:, 0:tot]).then_inc(T.sem.ln, 16)
+        nload += 16
+
+    g.wait_ge(T.sem.ln, nload)
+    for call in nh_calls(C, rank):
+        trs = []
+        for d, m in call:
+            w = C[rank][d]
+            yo = sum(C[s][d] for s in range(rank))
+            trs.append(RemoteDMATransfer(dst_ids=[did(cores[d])], dma_engine_mask=m, remote_sem=T.sem.nh,
+                                         src=T.xs[:, xoff[d]:xoff[d] + w], dst=T.land[:, yo:yo + w]))
+            sent += bits(m)
+        g.remote_dma_fused(trs, local_sem=T.sem.snt)
+
+    if rank != HOT:
+        due = 0
+        for s in range(n):
+            for call in nh_calls(C, s):
+                for d, m in call:
+                    if d == rank:
+                        due += bits(m)
+        ytot = sum(C[s][rank] for s in range(n))
+        g.sync.wait_ge(T.sem.nh, due)
+        g.sync.dma_start(T.y[:, 0:ytot], T.land[:, 0:ytot]).then_inc(T.sem.st, 16)
+        g.wait_ge(T.sem.snt, sent)
+        g.wait_ge(T.sem.st, 16)
+        return
+
+    qs = [g.sync, g.scalar]
+    nst = 0
+    whole = [s for s in srcs if s not in RELAY]
+    part = [s for s in srcs if s in RELAY]
+    for i, s in enumerate(part):
+        p = pos[s]
+        a = NQ - RELAY[s][1]
+        q = qs[i % 2]
+        q.wait_ge(T.sem["hd%d" % p], 2 * a)
+        q.dma_start(T.y[0:32 * a, p * W:(p + 1) * W], T["hl%d" % p][0:a]).then_inc(T.sem.st, 16)
+        nst += 16
+    for i, s in enumerate(part):
+        p = pos[s]
+        a = NQ - RELAY[s][1]
+        q = qs[i % 2]
+        q.wait_ge(T.sem["hr%d" % p], 8)
+        q.dma_start(T.y[32 * a:128, p * W:(p + 1) * W], T["hl%d" % p][a:NQ]).then_inc(T.sem.st, 16)
+        nst += 16
+    ng = 0
+    for s in whole:
+        p = pos[s]
+        g.wait_ge(T.sem["hd%d" % p], 2 * NQ)
+        g.dma_start(T.y[:, p * W:(p + 1) * W], T["hl%d" % p][:]).then_inc(T.sem.sg, 16)
+        ng += 16
+    g.wait_ge(T.sem.snt, sent)
+    g.wait_ge(T.sem.sg, ng)
+    g.wait_ge(T.sem.st, nst)

@@ -2,9 +2,10 @@ from concourse.bass import DstId, RemoteDMATransfer
 
 HOT = 6
 NQ = 4
-RELAY = {0: (62, 2), 2: (62, 2), 3: (63, 2), 4: (63, 1), 1: (59, 2), 5: (59, 1)}
+RELAY = {0: (62, 1), 2: (62, 1), 4: (63, 1), 1: (63, 1), 3: (59, 1), 5: (59, 1)}
 HOTMASK = [0x03, 0x0C, 0x30, 0xC0]
 MASKS = {1: [0xFF], 2: [0x0F, 0xF0], 3: [0x0F, 0x30, 0xC0], 4: [0x03, 0x0C, 0x30, 0xC0]}
+ON_G = [7]
 
 SCRATCH = {
     "hs": ("dram", [NQ, 128, 128], "float32"),
@@ -46,10 +47,6 @@ def rank_program(g, core, T, topo):
     def did(c):
         a = topo.addr(c)
         return DstId(rid=a[0], pnc=a[1])
-
-    def send(trs):
-        g.remote_dma_fused(trs, local_sem=T.sem.snt)
-        return sum(bits(t[0]) for t in trs) if False else 0
 
     if rank is None:
         mine = [s for s in srcs if s in RELAY and RELAY[s][0] == core]
@@ -127,24 +124,23 @@ def rank_program(g, core, T, topo):
 
     qs = [g.sync, g.scalar]
     nst = 0
-    whole = [s for s in srcs if s not in RELAY]
-    part = [s for s in srcs if s in RELAY]
-    for i, s in enumerate(part):
+    ng = 0
+    others = [s for s in srcs if s not in ON_G]
+    for i, s in enumerate(others):
         p = pos[s]
-        a = NQ - RELAY[s][1]
+        a = NQ - (RELAY[s][1] if s in RELAY else 0)
         q = qs[i % 2]
         q.wait_ge(T.sem["hd%d" % p], 2 * a)
         q.dma_start(T.y[0:32 * a, p * W:(p + 1) * W], T["hl%d" % p][0:a]).then_inc(T.sem.st, 16)
         nst += 16
-    for i, s in enumerate(part):
+    for i, s in enumerate([s for s in others if s in RELAY]):
         p = pos[s]
         a = NQ - RELAY[s][1]
         q = qs[i % 2]
         q.wait_ge(T.sem["hr%d" % p], 8)
         q.dma_start(T.y[32 * a:128, p * W:(p + 1) * W], T["hl%d" % p][a:NQ]).then_inc(T.sem.st, 16)
         nst += 16
-    ng = 0
-    for s in whole:
+    for s in ON_G:
         p = pos[s]
         g.wait_ge(T.sem["hd%d" % p], 2 * NQ)
         g.dma_start(T.y[:, p * W:(p + 1) * W], T["hl%d" % p][:]).then_inc(T.sem.sg, 16)

@@ -2,9 +2,9 @@ from concourse.bass import DstId, RemoteDMATransfer
 
 HOT = 6
 NQ = 4
-RELAY = {0: (62, 1), 2: (62, 1), 4: (63, 1), 1: (63, 1), 3: (59, 1), 5: (59, 1)}
-HOTMASK = [0x03, 0x0C, 0x30, 0xC0]
-MASKS = {1: [0xFF], 2: [0x0F, 0xF0], 3: [0x0F, 0x30, 0xC0], 4: [0x03, 0x0C, 0x30, 0xC0]}
+RSLOT = 1
+RELAY = {0: 62, 2: 62, 4: 63, 1: 63, 3: 59, 5: 59}
+WAVES = [[(0, 0x03), (1, 0x0C)], [(2, 0x0F)], [(3, 0x0F)]]
 ON_G = [7]
 
 SCRATCH = {
@@ -15,7 +15,7 @@ SCRATCH = {
 for i in range(7):
     SCRATCH["hl%d" % i] = ("dram", [NQ, 128, 128], "float32")
 
-SEMAPHORES = ["lh", "ln", "snt", "nh", "st", "sg"] + ["hd%d" % i for i in range(7)] + ["hr%d" % i for i in range(7)]
+SEMAPHORES = ["lh0", "lh1", "ln", "snt", "nh", "st", "sg"] + ["h%d_%d" % (i, j) for i in range(7) for j in range(NQ)]
 
 
 def bits(m):
@@ -30,7 +30,16 @@ def nh_calls(C, s):
     calls = []
     for w in sorted(groups, reverse=True):
         ds = groups[w]
-        calls.append(list(zip(ds, MASKS[len(ds)])))
+        if s == HOT:
+            calls.append(list(zip(ds, {1: [0xFF], 2: [0x0F, 0xF0], 3: [0x0F, 0x30, 0xC0]}[len(ds)])))
+        elif len(ds) == 4:
+            calls.append(list(zip(ds, [0x10, 0x20, 0x40, 0x80])))
+        else:
+            while len(ds) >= 2:
+                calls.append(list(zip(ds[:2], [0x30, 0xC0])))
+                ds = ds[2:]
+            if ds:
+                calls.append([(ds[0], 0xF0)])
     return calls
 
 
@@ -43,72 +52,73 @@ def rank_program(g, core, T, topo):
     srcs = [s for s in range(n) if C[s][HOT] > 0]
     pos = {s: i for i, s in enumerate(srcs)}
     W = C[srcs[0]][HOT]
+    eng = {j: bits(m) for wave in WAVES for j, m in wave}
 
     def did(c):
         a = topo.addr(c)
         return DstId(rid=a[0], pnc=a[1])
 
     if rank is None:
-        mine = [s for s in srcs if s in RELAY and RELAY[s][0] == core]
+        mine = [s for s in srcs if s in RELAY and RELAY[s] == core]
         if not mine:
             return
-        sent = 0
+        a = topo.addr(hotcore)
         for s in mine:
-            k = RELAY[s][1]
             p = pos[s]
             buf = T["hl%d" % p]
-            g.wait_ge(T.sem["hd%d" % p], 2 * k)
-            trs = []
-            for i in range(k):
-                j = NQ - k + i
-                trs.append(RemoteDMATransfer(dst_ids=[did(hotcore)], dma_engine_mask=MASKS[k][i],
-                                             remote_sem=T.sem["hr%d" % p], src=buf[j], dst=buf[j]))
-            g.remote_dma_fused(trs, local_sem=T.sem.snt)
-            sent += 8
-        g.wait_ge(T.sem.snt, sent)
+            sem = T.sem["h%d_%d" % (p, RSLOT)]
+            g.wait_ge(sem, eng[RSLOT])
+            g.remote_dma(buf[RSLOT], buf[RSLOT], sem, T.sem.snt, a[1], a[0], 0xFF)
+        g.wait_ge(T.sem.snt, 8 * len(mine))
         return
 
     xoff = [sum(C[rank][:d]) for d in range(n)]
     tot = sum(C[rank])
-    sent = 0
+    sent = [0]
 
-    nload = 0
-    if rank != HOT:
-        h = xoff[HOT]
-        g.sync.dma_start(T.hs[0:2], T.x[0:64, h:h + W]).then_inc(T.sem.lh, 16)
-        g.scalar.dma_start(T.hs[2:4], T.x[64:128, h:h + W]).then_inc(T.sem.lh, 16)
-        if h > 0:
-            g.sync.dma_start(T.xs[:, 0:h], T.x[:, 0:h]).then_inc(T.sem.ln, 16)
-            nload += 16
-        if tot > h + W:
-            g.scalar.dma_start(T.xs[:, h + W:tot], T.x[:, h + W:tot]).then_inc(T.sem.ln, 16)
-            nload += 16
-        p = pos[rank]
-        k = RELAY[rank][1] if rank in RELAY else 0
-        g.wait_ge(T.sem.lh, 32)
-        trs = []
-        for j in range(NQ):
-            to = hotcore if j < NQ - k else RELAY[rank][0]
-            trs.append(RemoteDMATransfer(dst_ids=[did(to)], dma_engine_mask=HOTMASK[j],
-                                         remote_sem=T.sem["hd%d" % p], src=T.hs[j], dst=T["hl%d" % p][j]))
-            sent += bits(HOTMASK[j])
-        g.remote_dma_fused(trs, local_sem=T.sem.snt)
-    else:
-        g.sync.dma_start(T.xs[:, 0:tot], T.x[:, 0:tot]).then_inc(T.sem.ln, 16)
-        nload += 16
-
-    g.wait_ge(T.sem.ln, nload)
-    for call in nh_calls(C, rank):
+    def other(call):
         trs = []
         for d, m in call:
             w = C[rank][d]
             yo = sum(C[s][d] for s in range(rank))
             trs.append(RemoteDMATransfer(dst_ids=[did(cores[d])], dma_engine_mask=m, remote_sem=T.sem.nh,
                                          src=T.xs[:, xoff[d]:xoff[d] + w], dst=T.land[:, yo:yo + w]))
-            sent += bits(m)
+            sent[0] += bits(m)
         g.remote_dma_fused(trs, local_sem=T.sem.snt)
 
+    def hot(wave):
+        p = pos[rank]
+        trs = []
+        for j, m in wave:
+            to = RELAY[rank] if (j == RSLOT and rank in RELAY) else hotcore
+            trs.append(RemoteDMATransfer(dst_ids=[did(to)], dma_engine_mask=m, remote_sem=T.sem["h%d_%d" % (p, j)],
+                                         src=T.hs[j], dst=T["hl%d" % p][j]))
+            sent[0] += bits(m)
+        g.remote_dma_fused(trs, local_sem=T.sem.snt)
+
+    calls = nh_calls(C, rank)
+
     if rank != HOT:
+        h = xoff[HOT]
+        nload = 0
+        g.sync.dma_start(T.hs[0:2], T.x[0:64, h:h + W]).then_inc(T.sem.lh0, 16)
+        g.sync.dma_start(T.hs[2:4], T.x[64:128, h:h + W]).then_inc(T.sem.lh1, 16)
+        if h > 0:
+            g.scalar.dma_start(T.xs[:, 0:h], T.x[:, 0:h]).then_inc(T.sem.ln, 16)
+            nload += 16
+        if tot > h + W:
+            g.scalar.dma_start(T.xs[:, h + W:tot], T.x[:, h + W:tot]).then_inc(T.sem.ln, 16)
+            nload += 16
+        g.wait_ge(T.sem.lh0, 16)
+        hot(WAVES[0])
+        g.wait_ge(T.sem.ln, nload)
+        other(calls[0])
+        g.wait_ge(T.sem.lh1, 16)
+        hot(WAVES[1])
+        other(calls[1])
+        hot(WAVES[2])
+        for call in calls[2:]:
+            other(call)
         due = 0
         for s in range(n):
             for call in nh_calls(C, s):
@@ -118,33 +128,33 @@ def rank_program(g, core, T, topo):
         ytot = sum(C[s][rank] for s in range(n))
         g.sync.wait_ge(T.sem.nh, due)
         g.sync.dma_start(T.y[:, 0:ytot], T.land[:, 0:ytot]).then_inc(T.sem.st, 16)
-        g.wait_ge(T.sem.snt, sent)
+        g.wait_ge(T.sem.snt, sent[0])
         g.wait_ge(T.sem.st, 16)
         return
 
+    g.sync.dma_start(T.xs[:, 0:tot], T.x[:, 0:tot]).then_inc(T.sem.ln, 16)
+    g.wait_ge(T.sem.ln, 16)
+    for call in calls:
+        other(call)
+
+    def store(q, sem, s, j0, j1, vals):
+        p = pos[s]
+        for j in range(j0, j1):
+            q.wait_ge(T.sem["h%d_%d" % (p, j)], vals[j - j0])
+        q.dma_start(T.y[32 * j0:32 * j1, p * W:(p + 1) * W], T["hl%d" % p][j0:j1]).then_inc(sem, 16)
+
     qs = [g.sync, g.scalar]
     nst = 0
-    ng = 0
     others = [s for s in srcs if s not in ON_G]
-    for i, s in enumerate(others):
-        p = pos[s]
-        a = NQ - (RELAY[s][1] if s in RELAY else 0)
-        q = qs[i % 2]
-        q.wait_ge(T.sem["hd%d" % p], 2 * a)
-        q.dma_start(T.y[0:32 * a, p * W:(p + 1) * W], T["hl%d" % p][0:a]).then_inc(T.sem.st, 16)
-        nst += 16
-    for i, s in enumerate([s for s in others if s in RELAY]):
-        p = pos[s]
-        a = NQ - RELAY[s][1]
-        q = qs[i % 2]
-        q.wait_ge(T.sem["hr%d" % p], 8)
-        q.dma_start(T.y[32 * a:128, p * W:(p + 1) * W], T["hl%d" % p][a:NQ]).then_inc(T.sem.st, 16)
-        nst += 16
+    for j, val in ((0, eng[0]), (2, eng[2]), (RSLOT, 8), (3, eng[3])):
+        for i, s in enumerate(others):
+            store(qs[i % 2], T.sem.st, s, j, j + 1, [val])
+            nst += 16
+    ng = 0
     for s in ON_G:
-        p = pos[s]
-        g.wait_ge(T.sem["hd%d" % p], 2 * NQ)
-        g.dma_start(T.y[:, p * W:(p + 1) * W], T["hl%d" % p][:]).then_inc(T.sem.sg, 16)
-        ng += 16
-    g.wait_ge(T.sem.snt, sent)
-    g.wait_ge(T.sem.sg, ng)
+        for j0, j1 in ((0, 2), (2, 3), (3, 4)):
+            store(g, T.sem["sg"], s, j0, j1, [eng[j] for j in range(j0, j1)])
+            ng += 16
+            g.wait_ge(T.sem.sg, ng)
+    g.wait_ge(T.sem.snt, sent[0])
     g.wait_ge(T.sem.st, nst)

@@ -5,6 +5,7 @@ NQ = 4
 RSLOT = 1
 RELAY = {0: 62, 2: 62, 4: 63, 1: 63, 3: 59, 5: 59}
 WAVES = [[(0, 0x03), (1, 0x0C)], [(2, 0x0F)], [(3, 0x0F)]]
+ORDER = "HNHNHN"
 ON_G = [7]
 
 SCRATCH = {
@@ -109,16 +110,19 @@ def rank_program(g, core, T, topo):
         if tot > h + W:
             g.scalar.dma_start(T.xs[:, h + W:tot], T.x[:, h + W:tot]).then_inc(T.sem.ln, 16)
             nload += 16
-        g.wait_ge(T.sem.lh0, 16)
-        hot(WAVES[0])
-        g.wait_ge(T.sem.ln, nload)
-        other(calls[0])
-        g.wait_ge(T.sem.lh1, 16)
-        hot(WAVES[1])
-        other(calls[1])
-        hot(WAVES[2])
-        for call in calls[2:]:
-            other(call)
+        nh = 0
+        nn = 0
+        for c in ORDER:
+            if c == "H":
+                if nh < 2:
+                    g.wait_ge(T.sem["lh%d" % nh], 16)
+                hot(WAVES[nh])
+                nh += 1
+            elif nn < len(calls):
+                if nn == 0:
+                    g.wait_ge(T.sem.ln, nload)
+                other(calls[nn])
+                nn += 1
         due = 0
         for s in range(n):
             for call in nh_calls(C, s):

from concourse.bass import DstId, RemoteDMATransfer

HOT = 6
NQ = 4
RSLOT = 1
RELAY = {0: 62, 2: 62, 4: 63, 1: 63, 3: 59, 5: 59}
WAVES = [[(0, 0x03), (1, 0x0C)], [(2, 0x0F)], [(3, 0x0F)]]
ORDER = "HNHNHN"
ON_G = [7]

SCRATCH = {
    "hs": ("dram", [NQ, 128, 128], "float32"),
    "xs": ("sbuf", [128, 1088], "float32"),
    "land": ("sbuf", [128, 640], "float32"),
}
for i in range(7):
    SCRATCH["hl%d" % i] = ("dram", [NQ, 128, 128], "float32")

SEMAPHORES = ["lh0", "lh1", "ln", "snt", "nh", "st", "sg"] + ["h%d_%d" % (i, j) for i in range(7) for j in range(NQ)]


def bits(m):
    return bin(m).count("1")


def nh_calls(C, s):
    groups = {}
    for d in range(len(C)):
        if d != HOT and C[s][d] > 0:
            groups.setdefault(C[s][d], []).append(d)
    calls = []
    for w in sorted(groups, reverse=True):
        ds = groups[w]
        if s == HOT:
            calls.append(list(zip(ds, {1: [0xFF], 2: [0x0F, 0xF0], 3: [0x0F, 0x30, 0xC0]}[len(ds)])))
        elif len(ds) == 4:
            calls.append(list(zip(ds, [0x10, 0x20, 0x40, 0x80])))
        else:
            while len(ds) >= 2:
                calls.append(list(zip(ds[:2], [0x30, 0xC0])))
                ds = ds[2:]
            if ds:
                calls.append([(ds[0], 0xF0)])
    return calls


def rank_program(g, core, T, topo):
    C = T.tables["COUNTS"]
    cores = T.cores
    n = len(cores)
    hotcore = cores[HOT]
    rank = T.rank_of(core)
    srcs = [s for s in range(n) if C[s][HOT] > 0]
    pos = {s: i for i, s in enumerate(srcs)}
    W = C[srcs[0]][HOT]
    eng = {j: bits(m) for wave in WAVES for j, m in wave}

    def did(c):
        a = topo.addr(c)
        return DstId(rid=a[0], pnc=a[1])

    if rank is None:
        mine = [s for s in srcs if s in RELAY and RELAY[s] == core]
        if not mine:
            return
        a = topo.addr(hotcore)
        for s in mine:
            p = pos[s]
            buf = T["hl%d" % p]
            sem = T.sem["h%d_%d" % (p, RSLOT)]
            g.wait_ge(sem, eng[RSLOT])
            g.remote_dma(buf[RSLOT], buf[RSLOT], sem, T.sem.snt, a[1], a[0], 0xFF)
        g.wait_ge(T.sem.snt, 8 * len(mine))
        return

    xoff = [sum(C[rank][:d]) for d in range(n)]
    tot = sum(C[rank])
    sent = [0]

    def other(call):
        trs = []
        for d, m in call:
            w = C[rank][d]
            yo = sum(C[s][d] for s in range(rank))
            trs.append(RemoteDMATransfer(dst_ids=[did(cores[d])], dma_engine_mask=m, remote_sem=T.sem.nh,
                                         src=T.xs[:, xoff[d]:xoff[d] + w], dst=T.land[:, yo:yo + w]))
            sent[0] += bits(m)
        g.remote_dma_fused(trs, local_sem=T.sem.snt)

    def hot(wave):
        p = pos[rank]
        trs = []
        for j, m in wave:
            to = RELAY[rank] if (j == RSLOT and rank in RELAY) else hotcore
            trs.append(RemoteDMATransfer(dst_ids=[did(to)], dma_engine_mask=m, remote_sem=T.sem["h%d_%d" % (p, j)],
                                         src=T.hs[j], dst=T["hl%d" % p][j]))
            sent[0] += bits(m)
        g.remote_dma_fused(trs, local_sem=T.sem.snt)

    calls = nh_calls(C, rank)

    if rank != HOT:
        h = xoff[HOT]
        nload = 0
        g.sync.dma_start(T.hs[0:2], T.x[0:64, h:h + W]).then_inc(T.sem.lh0, 16)
        g.sync.dma_start(T.hs[2:4], T.x[64:128, h:h + W]).then_inc(T.sem.lh1, 16)
        if h > 0:
            g.scalar.dma_start(T.xs[:, 0:h], T.x[:, 0:h]).then_inc(T.sem.ln, 16)
            nload += 16
        if tot > h + W:
            g.scalar.dma_start(T.xs[:, h + W:tot], T.x[:, h + W:tot]).then_inc(T.sem.ln, 16)
            nload += 16
        nh = 0
        nn = 0
        for c in ORDER:
            if c == "H":
                if nh < 2:
                    g.wait_ge(T.sem["lh%d" % nh], 16)
                hot(WAVES[nh])
                nh += 1
            elif nn < len(calls):
                if nn == 0:
                    g.wait_ge(T.sem.ln, nload)
                other(calls[nn])
                nn += 1
        due = 0
        for s in range(n):
            for call in nh_calls(C, s):
                for d, m in call:
                    if d == rank:
                        due += bits(m)
        ytot = sum(C[s][rank] for s in range(n))
        g.sync.wait_ge(T.sem.nh, due)
        g.sync.dma_start(T.y[:, 0:ytot], T.land[:, 0:ytot]).then_inc(T.sem.st, 16)
        g.wait_ge(T.sem.snt, sent[0])
        g.wait_ge(T.sem.st, 16)
        return

    g.sync.dma_start(T.xs[:, 0:tot], T.x[:, 0:tot]).then_inc(T.sem.ln, 16)
    g.wait_ge(T.sem.ln, 16)
    for call in calls:
        other(call)

    def store(q, sem, s, j0, j1, vals):
        p = pos[s]
        for j in range(j0, j1):
            q.wait_ge(T.sem["h%d_%d" % (p, j)], vals[j - j0])
        q.dma_start(T.y[32 * j0:32 * j1, p * W:(p + 1) * W], T["hl%d" % p][j0:j1]).then_inc(sem, 16)

    qs = [g.sync, g.scalar]
    nst = 0
    others = [s for s in srcs if s not in ON_G]
    for j, val in ((0, eng[0]), (2, eng[2]), (RSLOT, 8), (3, eng[3])):
        for i, s in enumerate(others):
            store(qs[i % 2], T.sem.st, s, j, j + 1, [val])
            nst += 16
    ng = 0
    for s in ON_G:
        for j0, j1 in ((0, 2), (2, 3), (3, 4)):
            store(g, T.sem["sg"], s, j0, j1, [eng[j] for j in range(j0, j1)])
            ng += 16
            g.wait_ge(T.sem.sg, ng)
    g.wait_ge(T.sem.snt, sent[0])
    g.wait_ge(T.sem.st, nst)
